import numpy as np
import ml_dtypes


def mxq(x, axis, fmt="e4m3"):
    dtype, down = {"e4m3": (ml_dtypes.float8_e4m3fn, 7), "e5m2": (ml_dtypes.float8_e5m2, 14)}[fmt]
    v = np.moveaxis(np.asarray(x, np.float32).astype(ml_dtypes.bfloat16).astype(np.float64), axis, -1)
    blocks = v.reshape(v.shape[:-1] + (-1, 32))
    amax = np.abs(blocks).max(-1, keepdims=True)
    byte = np.maximum(np.where(amax > 0, np.frexp(amax)[1] - 1 + 127, 0) - down, 1)
    scale = np.exp2(byte - 127.0)
    codes = (blocks / scale).astype(np.float32).astype(dtype).astype(np.float64)
    return np.moveaxis((codes * scale).reshape(v.shape), -1, axis)


WIDE = False


def mx_kscale(k):
    if not WIDE:
        return np.ones(k)
    levels = np.array([10, -10, 5, -5, 0])
    if k % 512:
        return np.exp2(np.random.permutation(np.resize(levels, k // 32))).repeat(32)
    a = np.empty((k // 512, 16))
    for p in range(k // 512):
        a[p, :8] = np.random.permutation(np.resize(levels, 8))
        for g in range(8):
            far = levels[np.abs(levels - a[p, g]) >= 10]
            a[p, g + 8] = far[np.random.randint(len(far))]
    return np.exp2(a.ravel()).repeat(32)


def f64(x):
    return np.asarray(x).astype(np.float64)


def striped(idx):
    return np.tile(np.asarray(idx).reshape(-1, 16).T, (8, 1)).astype(np.uint16)


def unstriped(offs):
    return offs[:16].T.reshape(-1).astype(np.int64)


O, G, T, D, M = 2, 1024, 4096, 512, 512


def setup_inputs():
    n = np.random.standard_normal
    s = mx_kscale(D)[:, None]
    grid = lambda x: np.round(x * 32) / 32
    return {
        "cb": (grid(n((O, D, T))) / s).astype(np.float32),
        "w": (n((D, M)) * s / np.sqrt(O * D)).astype(np.float32),
        "norm": np.tile(np.random.randint(32, 129, G) / 64.0, (128, 1)).astype(np.float32),
        "bias": (0.3 * n((M, 1))).astype(np.float32),
        "offs": striped(np.random.randint(0, T, O * G)),
    }


def reference(cb, w, norm, bias, offs):
    code = unstriped(offs).reshape(O, G)
    e = sum(f64(cb)[o][:, code[o]] for o in range(O)) * f64(norm)[:1]
    y = mxq(f64(w), 0, "e4m3").T @ mxq(e, 0, "e4m3")
    y = y + f64(bias)
    return y

@@ -1,0 +1,217 @@
+from contextlib import ExitStack
+
+import concourse.mybir as mybir
+from concourse.masks import make_identity
+
+O, D, T, G, M = 2, 512, 4096, 1024, 512
+P = 128
+PACK = 4
+HALF = M // 2
+
+FLOPS = 2 * M * D * G
+BYTES = 4 * (O * D * T + D * M + G + M + M * G) + 2 * 128 * 128
+
+F32 = mybir.dt.float32
+BF16 = mybir.dt.bfloat16
+U32 = mybir.dt.uint32
+U16 = mybir.dt.uint16
+U8 = mybir.dt.uint8
+FP8X4 = mybir.dt.float8_e4m3fn_x4
+IDENTITY = mybir.ActivationFunctionType.Identity
+MULT = mybir.AluOpType.mult
+ADD = mybir.AluOpType.add
+
+PIECES = ((0, 256), (256, 256), (512, 256), (768, 128), (896, 128))
+ON_VECTOR = ((1, 3), (3, 1), (3, 3), (4, 1), (4, 3))
+
+
+def tile_attend_aq_bias_kernel(tc, cb, w, norm, bias, offs, out):
+    nc = tc.nc
+    with ExitStack() as ctx:
+        hold = ctx.enter_context(tc.tile_pool(name="hold", bufs=1))
+        ring = ctx.enter_context(tc.tile_pool(name="ring", bufs=2))
+        psum = ctx.enter_context(tc.psum_pool(name="psum", bufs=8))
+
+        offsets = hold.tile([P, O * G // 16], U16, name="offsets")
+
+        tables = {}
+
+        def load_table(o, t):
+            table = hold.tile([P, T], F32, name="table_%d_%d" % (o, t))
+            nc.sync.dma_start(table[:], cb[o].rearrange("(p t) c -> p t c", t=PACK)[:, t, :])
+            tables[o, t] = table
+
+        w_raw = [hold.tile([P, PACK, HALF], F32, name="w_raw_%d" % h) for h in range(2)]
+
+        def load_w(h):
+            nc.sync.dma_start(w_raw[h][:], w.rearrange("(p t) m -> p t m", t=PACK)[:, :, h * HALF : (h + 1) * HALF])
+
+        bias_rows = hold.tile([P, P], F32, name="bias_rows")
+        nc.gpsimd.memset(bias_rows[:], 0.0)
+        norm_cols = hold.tile([P, G // P], F32, name="norm_cols")
+
+        nc.scalar.dma_start(norm_cols[:], norm[0:1, :].rearrange("o (p c) -> (o p) c", c=G // P))
+        nc.scalar.dma_start(bias_rows[0 : M // P, :], bias.rearrange("(b p) o -> b (p o)", p=P))
+        load_table(0, 0)
+        nc.sync.dma_start(offsets[:], offs)
+        load_table(1, 0)
+        load_table(0, 1)
+        load_table(1, 1)
+        load_table(0, 2)
+        load_table(1, 2)
+        load_table(0, 3)
+        load_table(1, 3)
+        load_w(0)
+        load_w(1)
+
+        ident = hold.tile([P, P], F32, name="ident")
+        make_identity(nc, ident[:])
+
+        norm_all = hold.tile([P, G], F32, name="norm_all")
+        for b in range(2):
+            turned = psum.tile([P, 4, P], F32, name="turned_%d" % b, tag="bank")
+            for c in range(4):
+                nc.tensor.transpose(turned[:, c, :], norm_cols[:, 4 * b + c : 4 * b + c + 1].to_broadcast([P, P]), ident[:])
+            nc.scalar.copy(
+                norm_all[:].rearrange("q (p c) -> q p c", c=8)[:, :, 4 * b : 4 * b + 4],
+                turned[:].rearrange("q c p -> q p c"),
+            )
+        bias_turned = psum.tile([P, P], F32, name="bias_turned", tag="bank")
+        nc.tensor.transpose(bias_turned[:], bias_rows[:], ident[:])
+        bias_cols = hold.tile([P, M // P], F32, name="bias_cols")
+        nc.scalar.copy(bias_cols[:], bias_turned[:, 0 : M // P])
+
+        w_codes = [hold.tile([P, HALF], U32, name="w_codes_%d" % h, align_bytes=64) for h in range(2)]
+        w_scales = [hold.tile([P, HALF], U8, name="w_scales_%d" % h, align_bytes=64) for h in range(2)]
+        w_groups = [hold.tile([P, HALF, PACK], BF16, name="w_groups_%d" % h, align_bytes=64) for h in range(2)]
+
+        def group_w(block):
+            h, b = divmod(block, 2)
+            copy = nc.vector.tensor_copy if block == 0 else nc.scalar.copy
+            copy(
+                w_groups[h][:, b * P : (b + 1) * P, :],
+                w_raw[h][:, :, b * P : (b + 1) * P].rearrange("p t m -> p m t"),
+            )
+
+        def quantise_w(h):
+            nc.vector.quantize_mx(
+                out=w_codes[h][:].bitcast(FP8X4),
+                scales=w_scales[h][:],
+                in_=w_groups[h][:].rearrange("p m t -> p (m t)"),
+            )
+
+        e_groups = hold.tile([P, G, PACK], BF16, name="e_groups", align_bytes=64)
+        e_codes = hold.tile([P, G], U32, name="e_codes", align_bytes=64)
+        e_scales = hold.tile([P, G], U8, name="e_scales", align_bytes=64)
+
+        def gather(o, t, dst, g, n):
+            nc.vector.tensor_tensor(
+                dst[:, g : g + n],
+                tables[o, t][:].indirect(offsets[:, (o * G + g) // 16 : (o * G + g + n) // 16]),
+                norm_all[:, g : g + n],
+                MULT,
+            )
+
+        def add(a, b, dst, g, n):
+            nc.vector.tensor_tensor(dst[:, g : g + n], a[:, g : g + n], b[:, g : g + n], ADD)
+
+        def place(src, t, g, n):
+            nc.vector.tensor_copy(e_groups[:, g : g + n, t], src[:, g : g + n])
+
+        for t in range(PACK - 1):
+            first = ring.tile([P, G], F32, name="first")
+            second = ring.tile([P, G], F32, name="second")
+            total = hold.tile([P, G], BF16, name="total")
+            gather(0, t, first, 0, G)
+            gather(1, t, second, 0, G)
+            add(first, second, total, 0, G)
+            nc.scalar.copy(e_groups[:, :, t], total[:])
+
+        last = PACK - 1
+        first = ring.tile([P, G], F32, name="first")
+        second = ring.tile([P, G], F32, name="second")
+        total = hold.tile([P, G], BF16, name="total")
+        gather(0, last, first, 0, G)
+
+        def quantise_e(g, n):
+            nc.vector.quantize_mx(
+                out=e_codes[:, g : g + n].bitcast(FP8X4),
+                scales=e_scales[:, g : g + n],
+                in_=e_groups[:, g : g + n, :].rearrange("p g t -> p (g t)"),
+            )
+
+        results = [hold.tile([P, 2, G], F32, name="results_%d" % h) for h in range(2)]
+
+        def multiply(i, h):
+            g, n = PIECES[i]
+            cols = slice(g, g + n)
+            for b in range(2):
+                block = 2 * h + b
+                acc = psum.tile([P, n], F32, name="acc", tag="bank")
+                nc.tensor.matmul_mx(
+                    out=acc[:],
+                    lhsT=w_codes[h][:, b * P : (b + 1) * P].bitcast(FP8X4),
+                    lhsT_scale=w_scales[h][:, b * P : (b + 1) * P],
+                    rhs=e_codes[:, cols].bitcast(FP8X4),
+                    rhs_scale=e_scales[:, cols],
+                    start=True,
+                    stop=True,
+                )
+                if (i, block) in ON_VECTOR:
+                    nc.vector.tensor_scalar_add(results[h][:, b, cols], acc[:], bias_cols[:, block : block + 1])
+                else:
+                    nc.scalar.activation(results[h][:, b, cols], acc[:], IDENTITY, bias=bias_cols[:, block : block + 1])
+            nc.sync.dma_start(
+                out[h * HALF : (h + 1) * HALF, cols].rearrange("(b p) g -> p b g", b=2), results[h][:, :, cols]
+            )
+
+        def gather_last(i):
+            gather(1, last, second, *PIECES[i])
+
+        def add_last(i):
+            add(first, second, total, *PIECES[i])
+
+        def place_last(i):
+            g, n = PIECES[i]
+            copy = nc.scalar.copy if i == 0 else nc.vector.tensor_copy
+            copy(e_groups[:, g : g + n, last], total[:, g : g + n])
+
+        def quantise_last(i):
+            quantise_e(*PIECES[i])
+
+        gather_last(0)
+        gather_last(1)
+        add_last(0)
+        group_w(1)
+        place_last(0)
+        group_w(2)
+        group_w(3)
+        group_w(0)
+        add_last(1)
+        gather_last(2)
+        quantise_w(0)
+        quantise_last(0)
+        multiply(0, 0)
+        place_last(1)
+        add_last(2)
+        quantise_last(1)
+        multiply(1, 0)
+        quantise_w(1)
+        multiply(0, 1)
+        place_last(2)
+        gather_last(3)
+        quantise_last(2)
+        multiply(1, 1)
+        add_last(3)
+        gather_last(4)
+        place_last(3)
+        add_last(4)
+        quantise_last(3)
+        multiply(2, 0)
+        multiply(2, 1)
+        place_last(4)
+        quantise_last(4)
+        multiply(3, 0)
+        multiply(3, 1)
+        multiply(4, 0)
+        multiply(4, 1)

@@ -22,7 +22,6 @@ MULT = mybir.AluOpType.mult
 ADD = mybir.AluOpType.add
 
 PIECES = ((0, 256), (256, 256), (512, 256), (768, 128), (896, 128))
-ON_VECTOR = ((1, 3), (3, 1), (3, 3), (4, 1), (4, 3))
 
 
 def tile_attend_aq_bias_kernel(tc, cb, w, norm, bias, offs, out):
@@ -55,12 +54,9 @@ def tile_attend_aq_bias_kernel(tc, cb, w, norm, bias, offs, out):
         load_table(0, 0)
         nc.sync.dma_start(offsets[:], offs)
         load_table(1, 0)
-        load_table(0, 1)
-        load_table(1, 1)
-        load_table(0, 2)
-        load_table(1, 2)
-        load_table(0, 3)
-        load_table(1, 3)
+        for t in range(1, PACK):
+            load_table(0, t)
+            load_table(1, t)
         load_w(0)
         load_w(1)
 
@@ -83,12 +79,11 @@ def tile_attend_aq_bias_kernel(tc, cb, w, norm, bias, offs, out):
 
         w_codes = [hold.tile([P, HALF], U32, name="w_codes_%d" % h, align_bytes=64) for h in range(2)]
         w_scales = [hold.tile([P, HALF], U8, name="w_scales_%d" % h, align_bytes=64) for h in range(2)]
-        w_groups = [hold.tile([P, HALF, PACK], BF16, name="w_groups_%d" % h, align_bytes=64) for h in range(2)]
+        w_groups = [hold.tile([P, HALF, PACK], BF16, name="w_groups_%d" % h, tag="stage_%d" % h, align_bytes=64) for h in range(2)]
 
         def group_w(block):
             h, b = divmod(block, 2)
-            copy = nc.vector.tensor_copy if block == 0 else nc.scalar.copy
-            copy(
+            nc.scalar.copy(
                 w_groups[h][:, b * P : (b + 1) * P, :],
                 w_raw[h][:, :, b * P : (b + 1) * P].rearrange("p t m -> p m t"),
             )
@@ -104,42 +99,23 @@ def tile_attend_aq_bias_kernel(tc, cb, w, norm, bias, offs, out):
         e_codes = hold.tile([P, G], U32, name="e_codes", align_bytes=64)
         e_scales = hold.tile([P, G], U8, name="e_scales", align_bytes=64)
 
-        def gather(o, t, dst, g, n):
-            nc.vector.tensor_tensor(
-                dst[:, g : g + n],
-                tables[o, t][:].indirect(offsets[:, (o * G + g) // 16 : (o * G + g + n) // 16]),
-                norm_all[:, g : g + n],
-                MULT,
-            )
-
-        def add(a, b, dst, g, n):
-            nc.vector.tensor_tensor(dst[:, g : g + n], a[:, g : g + n], b[:, g : g + n], ADD)
-
-        def place(src, t, g, n):
-            nc.vector.tensor_copy(e_groups[:, g : g + n, t], src[:, g : g + n])
+        def listed(o, t, g, n):
+            return tables[o, t][:].indirect(offsets[:, (o * G + g) // 16 : (o * G + g + n) // 16])
 
         for t in range(PACK - 1):
             first = ring.tile([P, G], F32, name="first")
-            second = ring.tile([P, G], F32, name="second")
-            total = hold.tile([P, G], BF16, name="total")
-            gather(0, t, first, 0, G)
-            gather(1, t, second, 0, G)
-            add(first, second, total, 0, G)
-            nc.scalar.copy(e_groups[:, :, t], total[:])
+            both = ring.tile([P, G], F32, name="both")
+            plane = hold.tile([P, G], BF16, name="plane")
+            nc.vector.tensor_copy(first[:], listed(0, t, 0, G))
+            nc.vector.tensor_tensor(both[:], listed(1, t, 0, G), first[:], ADD)
+            nc.vector.tensor_tensor(plane[:], both[:], norm_all[:], MULT)
+            nc.scalar.copy(e_groups[:, :, t], plane[:])
 
         last = PACK - 1
         first = ring.tile([P, G], F32, name="first")
-        second = ring.tile([P, G], F32, name="second")
-        total = hold.tile([P, G], BF16, name="total")
-        gather(0, last, first, 0, G)
+        nc.vector.tensor_copy(first[:], listed(0, last, 0, G))
 
-        def quantise_e(g, n):
-            nc.vector.quantize_mx(
-                out=e_codes[:, g : g + n].bitcast(FP8X4),
-                scales=e_scales[:, g : g + n],
-                in_=e_groups[:, g : g + n, :].rearrange("p g t -> p (g t)"),
-            )
-
+        plane = hold.tile([P, G], BF16, name="plane")
         results = [hold.tile([P, 2, G], F32, name="results_%d" % h) for h in range(2)]
 
         def multiply(i, h):
@@ -157,7 +133,7 @@ def tile_attend_aq_bias_kernel(tc, cb, w, norm, bias, offs, out):
                     start=True,
                     stop=True,
                 )
-                if (i, block) in ON_VECTOR:
+                if i >= len(PIECES) - 2 and b == 1:
                     nc.vector.tensor_scalar_add(results[h][:, b, cols], acc[:], bias_cols[:, block : block + 1])
                 else:
                     nc.scalar.activation(results[h][:, b, cols], acc[:], IDENTITY, bias=bias_cols[:, block : block + 1])
@@ -165,53 +141,35 @@ def tile_attend_aq_bias_kernel(tc, cb, w, norm, bias, offs, out):
                 out[h * HALF : (h + 1) * HALF, cols].rearrange("(b p) g -> p b g", b=2), results[h][:, :, cols]
             )
 
-        def gather_last(i):
-            gather(1, last, second, *PIECES[i])
-
-        def add_last(i):
-            add(first, second, total, *PIECES[i])
-
-        def place_last(i):
+        def make_piece(i):
             g, n = PIECES[i]
-            copy = nc.scalar.copy if i == 0 else nc.vector.tensor_copy
-            copy(e_groups[:, g : g + n, last], total[:, g : g + n])
+            cols = slice(g, g + n)
+            if i >= 2:
+                piece_sum = hold.tile([P, n], F32, name="piece_sum_%d" % i, tag="stage_%d" % (i % 2), align_bytes=64)
+            else:
+                piece_sum = ring.tile([P, n], F32, name="piece_sum")
+            nc.vector.tensor_tensor(piece_sum[:], listed(1, last, g, n), first[:, cols], ADD)
+            nc.vector.tensor_tensor(plane[:, cols], piece_sum[:], norm_all[:, cols], MULT)
+            nc.vector.tensor_copy(e_groups[:, cols, last], plane[:, cols])
+            nc.vector.quantize_mx(
+                out=e_codes[:, cols].bitcast(FP8X4),
+                scales=e_scales[:, cols],
+                in_=e_groups[:, cols, :].rearrange("p g t -> p (g t)"),
+            )
 
-        def quantise_last(i):
-            quantise_e(*PIECES[i])
-
-        gather_last(0)
-        gather_last(1)
-        add_last(0)
+        group_w(0)
         group_w(1)
-        place_last(0)
+        make_piece(0)
+        quantise_w(0)
+        multiply(0, 0)
         group_w(2)
         group_w(3)
-        group_w(0)
-        add_last(1)
-        gather_last(2)
-        quantise_w(0)
-        quantise_last(0)
-        multiply(0, 0)
-        place_last(1)
-        add_last(2)
-        quantise_last(1)
-        multiply(1, 0)
+        make_piece(1)
         quantise_w(1)
         multiply(0, 1)
-        place_last(2)
-        gather_last(3)
-        quantise_last(2)
+        multiply(1, 0)
         multiply(1, 1)
-        add_last(3)
-        gather_last(4)
-        place_last(3)
-        add_last(4)
-        quantise_last(3)
-        multiply(2, 0)
-        multiply(2, 1)
-        place_last(4)
-        quantise_last(4)
-        multiply(3, 0)
-        multiply(3, 1)
-        multiply(4, 0)
-        multiply(4, 1)
+        for i in range(2, len(PIECES)):
+            make_piece(i)
+            multiply(i, 0)
+            multiply(i, 1)

@@ -84,8 +84,8 @@ def tile_attend_aq_bias_kernel(tc, cb, w, norm, bias, offs, out):
         def group_w(block):
             h, b = divmod(block, 2)
             nc.scalar.copy(
-                w_groups[h][:, b * P : (b + 1) * P, :],
-                w_raw[h][:, :, b * P : (b + 1) * P].rearrange("p t m -> p m t"),
+                w_groups[h][:, b * P : (b + 1) * P, :].rearrange("p (c i) t -> p c t i", i=4),
+                w_raw[h][:, :, b * P : (b + 1) * P].rearrange("p t (c i) -> p c t i", i=4),
             )
 
         def quantise_w(h):
@@ -118,6 +118,10 @@ def tile_attend_aq_bias_kernel(tc, cb, w, norm, bias, offs, out):
         plane = hold.tile([P, G], BF16, name="plane")
         results = [hold.tile([P, 2, G], F32, name="results_%d" % h) for h in range(2)]
 
+        def store(h, b0, b1, g, n):
+            rows = out[h * HALF + b0 * P : h * HALF + b1 * P, g : g + n]
+            nc.sync.dma_start(rows.rearrange("(b p) g -> p b g", p=P), results[h][:, b0:b1, g : g + n])
+
         def multiply(i, h):
             g, n = PIECES[i]
             cols = slice(g, g + n)
@@ -133,13 +137,16 @@ def tile_attend_aq_bias_kernel(tc, cb, w, norm, bias, offs, out):
                     start=True,
                     stop=True,
                 )
-                if i >= len(PIECES) - 2 and b == 1:
+                if i >= len(PIECES) - 2 and h == 1:
                     nc.vector.tensor_scalar_add(results[h][:, b, cols], acc[:], bias_cols[:, block : block + 1])
                 else:
                     nc.scalar.activation(results[h][:, b, cols], acc[:], IDENTITY, bias=bias_cols[:, block : block + 1])
-            nc.sync.dma_start(
-                out[h * HALF : (h + 1) * HALF, cols].rearrange("(b p) g -> p b g", b=2), results[h][:, :, cols]
-            )
+                if i == 0:
+                    store(h, b, b + 1, g, n)
+                if i == len(PIECES) - 1:
+                    store(h, b, b + 1, g - n, 2 * n)
+            if 0 < i < len(PIECES) - 2:
+                store(h, 0, 2, g, n)
 
         def make_piece(i):
             g, n = PIECES[i]

@@ -148,35 +148,59 @@ def tile_attend_aq_bias_kernel(tc, cb, w, norm, bias, offs, out):
             if 0 < i < len(PIECES) - 2:
                 store(h, 0, 2, g, n)
 
-        def make_piece(i):
+        sums, planes = {}, {}
+
+        def gather(i):
             g, n = PIECES[i]
-            cols = slice(g, g + n)
-            if i >= 2:
-                piece_sum = hold.tile([P, n], F32, name="piece_sum_%d" % i, tag="stage_%d" % (i % 2), align_bytes=64)
-            else:
-                piece_sum = ring.tile([P, n], F32, name="piece_sum")
-            nc.vector.tensor_tensor(piece_sum[:], listed(1, last, g, n), first[:, cols], ADD)
-            nc.vector.tensor_tensor(plane[:, cols], piece_sum[:], norm_all[:, cols], MULT)
-            nc.vector.tensor_copy(e_groups[:, cols, last], plane[:, cols])
+            nc.vector.tensor_tensor(sums[i], listed(1, last, g, n), first[:, g : g + n], ADD)
+
+        def scale(i):
+            g, n = PIECES[i]
+            nc.vector.tensor_tensor(planes[i], sums[i], norm_all[:, g : g + n], MULT)
+
+        def place(i):
+            g, n = PIECES[i]
+            nc.vector.tensor_copy(e_groups[:, g : g + n, last], planes[i])
+
+        def quantise_e(i):
+            g, n = PIECES[i]
             nc.vector.quantize_mx(
-                out=e_codes[:, cols].bitcast(FP8X4),
-                scales=e_scales[:, cols],
-                in_=e_groups[:, cols, :].rearrange("p g t -> p (g t)"),
+                out=e_codes[:, g : g + n].bitcast(FP8X4),
+                scales=e_scales[:, g : g + n],
+                in_=e_groups[:, g : g + n, :].rearrange("p g t -> p (g t)"),
             )
 
-        group_w(0)
-        group_w(1)
-        make_piece(0)
+        early_sums = hold.tile([P, 512], F32, name="early_sums")
+        for i, (g, n) in enumerate(PIECES):
+            planes[i] = plane[:, g : g + n]
+        for block in range(4):
+            group_w(block)
+        for i in range(2):
+            sums[i] = early_sums[:, 256 * i : 256 * (i + 1)]
+            gather(i)
+        for step in (scale, place, quantise_e):
+            step(0)
+            step(1)
         quantise_w(0)
         multiply(0, 0)
-        group_w(2)
-        group_w(3)
-        make_piece(1)
+        multiply(1, 0)
+        middle = hold.tile([P, 256], F32, name="middle", tag="stage_0", align_bytes=64)
+        sums[2] = middle[:]
+        gather(2)
         quantise_w(1)
         multiply(0, 1)
-        multiply(1, 0)
         multiply(1, 1)
+        late = hold.tile([P, 384], F32, name="late", tag="stage_1", align_bytes=64)
+        sums[3] = late[:, 0:128]
+        sums[4] = late[:, 128:256]
+        planes[2] = late[:, 256:384].bitcast(BF16)
+        scale(2)
         for i in range(2, len(PIECES)):
-            make_piece(i)
+            if i + 1 < len(PIECES):
+                gather(i + 1)
+            place(i)
+            if i + 1 < len(PIECES):
+                scale(i + 1)
+            quantise_e(i)
             multiply(i, 0)
             multiply(i, 1)

@@ -6,10 +6,17 @@ from concourse.masks import make_identity
 O, D, T, G, M = 2, 512, 4096, 1024, 512
 P = 128
 PACK = 4
+LAST = PACK - 1
+BLOCKS = M // P
 HALF = M // 2
+LIST_ROWS = 16
+BANK = 512
+NORM_RUN = G // P
+PIECE = 256
+RUN = 4
 
 FLOPS = 2 * M * D * G
-BYTES = 4 * (O * D * T + D * M + G + M + M * G) + 2 * 128 * 128
+BYTES = 4 * (O * D * T + D * M + G + M + M * G) + 2 * P * (O * G // LIST_ROWS)
 
 F32 = mybir.dt.float32
 BF16 = mybir.dt.bfloat16
@@ -21,8 +28,6 @@ IDENTITY = mybir.ActivationFunctionType.Identity
 MULT = mybir.AluOpType.mult
 ADD = mybir.AluOpType.add
 
-PIECES = ((0, 256), (256, 256), (512, 256), (768, 128), (896, 128))
-
 
 def tile_attend_aq_bias_kernel(tc, cb, w, norm, bias, offs, out):
     nc = tc.nc
@@ -31,61 +36,55 @@ def tile_attend_aq_bias_kernel(tc, cb, w, norm, bias, offs, out):
         ring = ctx.enter_context(tc.tile_pool(name="ring", bufs=2))
         psum = ctx.enter_context(tc.psum_pool(name="psum", bufs=8))
 
-        offsets = hold.tile([P, O * G // 16], U16, name="offsets")
-
-        tables = {}
-
-        def load_table(o, t):
-            table = hold.tile([P, T], F32, name="table_%d_%d" % (o, t))
-            nc.sync.dma_start(table[:], cb[o].rearrange("(p t) c -> p t c", t=PACK)[:, t, :])
-            tables[o, t] = table
-
-        w_raw = [hold.tile([P, PACK, HALF], F32, name="w_raw_%d" % h) for h in range(2)]
-
-        def load_w(h):
-            nc.sync.dma_start(w_raw[h][:], w.rearrange("(p t) m -> p t m", t=PACK)[:, :, h * HALF : (h + 1) * HALF])
-
         bias_rows = hold.tile([P, P], F32, name="bias_rows")
         nc.gpsimd.memset(bias_rows[:], 0.0)
-        norm_cols = hold.tile([P, G // P], F32, name="norm_cols")
+        norm_runs = hold.tile([P, NORM_RUN], F32, name="norm_runs")
+        nc.scalar.dma_start(norm_runs[:], norm[0:1, :].rearrange("o (p c) -> (o p) c", c=NORM_RUN))
+        nc.scalar.dma_start(bias_rows[0:BLOCKS, :], bias.rearrange("(b p) o -> b (p o)", p=P))
 
-        nc.scalar.dma_start(norm_cols[:], norm[0:1, :].rearrange("o (p c) -> (o p) c", c=G // P))
-        nc.scalar.dma_start(bias_rows[0 : M // P, :], bias.rearrange("(b p) o -> b (p o)", p=P))
-        load_table(0, 0)
-        nc.sync.dma_start(offsets[:], offs)
-        load_table(1, 0)
-        for t in range(1, PACK):
-            load_table(0, t)
-            load_table(1, t)
-        load_w(0)
-        load_w(1)
+        offsets = hold.tile([P, O * G // LIST_ROWS], U16, name="offsets")
+        tables = {}
+        for t in range(PACK):
+            for o in range(O):
+                tables[o, t] = hold.tile([P, T], F32, name="table_%d_%d" % (o, t))
+                nc.sync.dma_start(tables[o, t][:], cb[o].rearrange("(p t) c -> p t c", t=PACK)[:, t, :])
+                if (o, t) == (0, 0):
+                    nc.sync.dma_start(offsets[:], offs)
+        w_raw = []
+        for h in range(2):
+            w_raw.append(hold.tile([P, PACK, HALF], F32, name="w_raw_%d" % h))
+            nc.sync.dma_start(w_raw[h][:], w.rearrange("(p t) m -> p t m", t=PACK)[:, :, h * HALF : (h + 1) * HALF])
 
         ident = hold.tile([P, P], F32, name="ident")
         make_identity(nc, ident[:])
 
         norm_all = hold.tile([P, G], F32, name="norm_all")
-        for b in range(2):
-            turned = psum.tile([P, 4, P], F32, name="turned_%d" % b, tag="bank")
-            for c in range(4):
-                nc.tensor.transpose(turned[:, c, :], norm_cols[:, 4 * b + c : 4 * b + c + 1].to_broadcast([P, P]), ident[:])
+        per_bank = BANK // P
+        for c0 in range(0, NORM_RUN, per_bank):
+            turned = psum.tile([P, per_bank, P], F32, name="turned", tag="bank")
+            for c in range(per_bank):
+                nc.tensor.transpose(turned[:, c, :], norm_runs[:, c0 + c : c0 + c + 1].to_broadcast([P, P]), ident[:])
             nc.scalar.copy(
-                norm_all[:].rearrange("q (p c) -> q p c", c=8)[:, :, 4 * b : 4 * b + 4],
+                norm_all[:].rearrange("q (p c) -> q p c", c=NORM_RUN)[:, :, c0 : c0 + per_bank],
                 turned[:].rearrange("q c p -> q p c"),
             )
         bias_turned = psum.tile([P, P], F32, name="bias_turned", tag="bank")
         nc.tensor.transpose(bias_turned[:], bias_rows[:], ident[:])
-        bias_cols = hold.tile([P, M // P], F32, name="bias_cols")
-        nc.scalar.copy(bias_cols[:], bias_turned[:, 0 : M // P])
+        bias_cols = hold.tile([P, BLOCKS], F32, name="bias_cols")
+        nc.scalar.copy(bias_cols[:], bias_turned[:, 0:BLOCKS])
 
         w_codes = [hold.tile([P, HALF], U32, name="w_codes_%d" % h, align_bytes=64) for h in range(2)]
         w_scales = [hold.tile([P, HALF], U8, name="w_scales_%d" % h, align_bytes=64) for h in range(2)]
-        w_groups = [hold.tile([P, HALF, PACK], BF16, name="w_groups_%d" % h, tag="stage_%d" % h, align_bytes=64) for h in range(2)]
+        w_groups = [
+            hold.tile([P, HALF, PACK], BF16, name="w_groups_%d" % h, tag="stage_%d" % h, align_bytes=64)
+            for h in range(2)
+        ]
 
         def group_w(block):
             h, b = divmod(block, 2)
             nc.scalar.copy(
-                w_groups[h][:, b * P : (b + 1) * P, :].rearrange("p (c i) t -> p c t i", i=4),
-                w_raw[h][:, :, b * P : (b + 1) * P].rearrange("p t (c i) -> p c t i", i=4),
+                w_groups[h][:, b * P : (b + 1) * P, :].rearrange("p (c i) t -> p c t i", i=RUN),
+                w_raw[h][:, :, b * P : (b + 1) * P].rearrange("p t (c i) -> p c t i", i=RUN),
             )
 
         def quantise_w(h):
@@ -100,9 +99,10 @@ def tile_attend_aq_bias_kernel(tc, cb, w, norm, bias, offs, out):
         e_scales = hold.tile([P, G], U8, name="e_scales", align_bytes=64)
 
         def listed(o, t, g, n):
-            return tables[o, t][:].indirect(offsets[:, (o * G + g) // 16 : (o * G + g + n) // 16])
+            entry = o * G + g
+            return tables[o, t][:].indirect(offsets[:, entry // LIST_ROWS : (entry + n) // LIST_ROWS])
 
-        for t in range(PACK - 1):
+        for t in range(LAST):
             first = ring.tile([P, G], F32, name="first")
             both = ring.tile([P, G], F32, name="both")
             plane = hold.tile([P, G], BF16, name="plane")
@@ -111,96 +111,86 @@ def tile_attend_aq_bias_kernel(tc, cb, w, norm, bias, offs, out):
             nc.vector.tensor_tensor(plane[:], both[:], norm_all[:], MULT)
             nc.scalar.copy(e_groups[:, :, t], plane[:])
 
-        last = PACK - 1
         first = ring.tile([P, G], F32, name="first")
-        nc.vector.tensor_copy(first[:], listed(0, last, 0, G))
-
+        nc.vector.tensor_copy(first[:], listed(0, LAST, 0, G))
         plane = hold.tile([P, G], BF16, name="plane")
-        results = [hold.tile([P, 2, G], F32, name="results_%d" % h) for h in range(2)]
 
-        def store(h, b0, b1, g, n):
-            rows = out[h * HALF + b0 * P : h * HALF + b1 * P, g : g + n]
-            nc.sync.dma_start(rows.rearrange("(b p) g -> p b g", p=P), results[h][:, b0:b1, g : g + n])
-
-        def multiply(i, h):
-            g, n = PIECES[i]
-            cols = slice(g, g + n)
-            for b in range(2):
-                block = 2 * h + b
-                acc = psum.tile([P, n], F32, name="acc", tag="bank")
-                nc.tensor.matmul_mx(
-                    out=acc[:],
-                    lhsT=w_codes[h][:, b * P : (b + 1) * P].bitcast(FP8X4),
-                    lhsT_scale=w_scales[h][:, b * P : (b + 1) * P],
-                    rhs=e_codes[:, cols].bitcast(FP8X4),
-                    rhs_scale=e_scales[:, cols],
-                    start=True,
-                    stop=True,
-                )
-                if i >= len(PIECES) - 2 and h == 1:
-                    nc.vector.tensor_scalar_add(results[h][:, b, cols], acc[:], bias_cols[:, block : block + 1])
-                else:
-                    nc.scalar.activation(results[h][:, b, cols], acc[:], IDENTITY, bias=bias_cols[:, block : block + 1])
-                if i == 0:
-                    store(h, b, b + 1, g, n)
-                if i == len(PIECES) - 1:
-                    store(h, b, b + 1, g - n, 2 * n)
-            if 0 < i < len(PIECES) - 2:
-                store(h, 0, 2, g, n)
-
-        sums, planes = {}, {}
+        sums = {}
+        rounded = {i: plane[:, i * PIECE : (i + 1) * PIECE] for i in range(G // PIECE)}
 
         def gather(i):
-            g, n = PIECES[i]
-            nc.vector.tensor_tensor(sums[i], listed(1, last, g, n), first[:, g : g + n], ADD)
+            nc.vector.tensor_tensor(sums[i], listed(1, LAST, i * PIECE, PIECE), first[:, i * PIECE : (i + 1) * PIECE], ADD)
 
         def scale(i):
-            g, n = PIECES[i]
-            nc.vector.tensor_tensor(planes[i], sums[i], norm_all[:, g : g + n], MULT)
+            nc.vector.tensor_tensor(rounded[i], sums[i], norm_all[:, i * PIECE : (i + 1) * PIECE], MULT)
 
         def place(i):
-            g, n = PIECES[i]
-            nc.vector.tensor_copy(e_groups[:, g : g + n, last], planes[i])
+            nc.vector.tensor_copy(e_groups[:, i * PIECE : (i + 1) * PIECE, LAST], rounded[i])
 
         def quantise_e(i):
-            g, n = PIECES[i]
+            cols = slice(i * PIECE, (i + 1) * PIECE)
             nc.vector.quantize_mx(
-                out=e_codes[:, g : g + n].bitcast(FP8X4),
-                scales=e_scales[:, g : g + n],
-                in_=e_groups[:, g : g + n, :].rearrange("p g t -> p (g t)"),
+                out=e_codes[:, cols].bitcast(FP8X4),
+                scales=e_scales[:, cols],
+                in_=e_groups[:, cols, :].rearrange("p g t -> p (g t)"),
             )
 
-        early_sums = hold.tile([P, 512], F32, name="early_sums")
-        for i, (g, n) in enumerate(PIECES):
-            planes[i] = plane[:, g : g + n]
-        for block in range(4):
+        results = hold.tile([P, BLOCKS, G], F32, name="results")
+
+        def multiply(block, g, n, on_vector=False):
+            h, b = divmod(block, 2)
+            acc = psum.tile([P, n], F32, name="acc", tag="bank")
+            nc.tensor.matmul_mx(
+                out=acc[:],
+                lhsT=w_codes[h][:, b * P : (b + 1) * P].bitcast(FP8X4),
+                lhsT_scale=w_scales[h][:, b * P : (b + 1) * P],
+                rhs=e_codes[:, g : g + n].bitcast(FP8X4),
+                rhs_scale=e_scales[:, g : g + n],
+                start=True,
+                stop=True,
+            )
+            if on_vector:
+                nc.vector.tensor_scalar_add(results[:, block, g : g + n], acc[:], bias_cols[:, block : block + 1])
+            else:
+                nc.scalar.activation(results[:, block, g : g + n], acc[:], IDENTITY, bias=bias_cols[:, block : block + 1])
+            nc.sync.dma_start(out[block * P : (block + 1) * P, g : g + n], results[:, block, g : g + n])
+
+        def multiply_first_pieces(h):
+            for i in range(2):
+                multiply(2 * h, i * PIECE, PIECE)
+            multiply(2 * h + 1, 0, 2 * PIECE)
+
+        for block in range(BLOCKS):
             group_w(block)
+
+        early_sums = hold.tile([P, 2, PIECE], F32, name="early_sums")
         for i in range(2):
-            sums[i] = early_sums[:, 256 * i : 256 * (i + 1)]
+            sums[i] = early_sums[:, i, :]
             gather(i)
         for step in (scale, place, quantise_e):
             step(0)
             step(1)
+
         quantise_w(0)
-        multiply(0, 0)
-        multiply(1, 0)
-        middle = hold.tile([P, 256], F32, name="middle", tag="stage_0", align_bytes=64)
+        multiply_first_pieces(0)
+        middle = hold.tile([P, PIECE], F32, name="middle", tag="stage_0", align_bytes=64)
         sums[2] = middle[:]
         gather(2)
         quantise_w(1)
-        multiply(0, 1)
-        multiply(1, 1)
-        late = hold.tile([P, 384], F32, name="late", tag="stage_1", align_bytes=64)
-        sums[3] = late[:, 0:128]
-        sums[4] = late[:, 128:256]
-        planes[2] = late[:, 256:384].bitcast(BF16)
+        multiply_first_pieces(1)
+        late = hold.tile([P, PIECE + PIECE // 2], F32, name="late", tag="stage_1", align_bytes=64)
+        sums[3] = late[:, 0:PIECE]
+        rounded[2] = late[:, PIECE:].bitcast(BF16)
+
         scale(2)
-        for i in range(2, len(PIECES)):
-            if i + 1 < len(PIECES):
-                gather(i + 1)
-            place(i)
-            if i + 1 < len(PIECES):
-                scale(i + 1)
-            quantise_e(i)
-            multiply(i, 0)
-            multiply(i, 1)
+        gather(3)
+        place(2)
+        scale(3)
+        quantise_e(2)
+        for block in range(BLOCKS):
+            multiply(block, 2 * PIECE, PIECE)
+        place(3)
+        quantise_e(3)
+        for block in range(2):
+            for lower in range(2):
+                multiply(block + 2 * lower, 3 * PIECE, PIECE, on_vector=lower == 1)

@@ -75,23 +75,23 @@ def tile_attend_aq_bias_kernel(tc, cb, w, norm, bias, offs, out):
 
         w_codes = [hold.tile([P, HALF], U32, name="w_codes_%d" % h, align_bytes=64) for h in range(2)]
         w_scales = [hold.tile([P, HALF], U8, name="w_scales_%d" % h, align_bytes=64) for h in range(2)]
-        w_groups = [
-            hold.tile([P, HALF, PACK], BF16, name="w_groups_%d" % h, tag="stage_%d" % h, align_bytes=64)
-            for h in range(2)
-        ]
+        w_first = hold.tile([P, HALF, PACK], BF16, name="w_first", tag="stage_0", align_bytes=64)
+        w_third = hold.tile([P, P, PACK], BF16, name="w_third", tag="stage_1", align_bytes=64)
+        w_fourth = hold.tile([P, P, PACK], BF16, name="w_fourth", align_bytes=64)
+        w_groups = [w_first[:, 0:P, :], w_first[:, P:HALF, :], w_third[:], w_fourth[:]]
 
         def group_w(block):
             h, b = divmod(block, 2)
             nc.scalar.copy(
-                w_groups[h][:, b * P : (b + 1) * P, :].rearrange("p (c i) t -> p c t i", i=RUN),
+                w_groups[block].rearrange("p (c i) t -> p c t i", i=RUN),
                 w_raw[h][:, :, b * P : (b + 1) * P].rearrange("p t (c i) -> p c t i", i=RUN),
             )
 
-        def quantise_w(h):
+        def quantise_w(h, cols, groups):
             nc.vector.quantize_mx(
-                out=w_codes[h][:].bitcast(FP8X4),
-                scales=w_scales[h][:],
-                in_=w_groups[h][:].rearrange("p m t -> p (m t)"),
+                out=w_codes[h][:, cols].bitcast(FP8X4),
+                scales=w_scales[h][:, cols],
+                in_=groups.rearrange("p m t -> p (m t)"),
             )
 
         e_groups = hold.tile([P, G, PACK], BF16, name="e_groups", align_bytes=64)
@@ -155,11 +155,6 @@ def tile_attend_aq_bias_kernel(tc, cb, w, norm, bias, offs, out):
                 nc.scalar.activation(results[:, block, g : g + n], acc[:], IDENTITY, bias=bias_cols[:, block : block + 1])
             nc.sync.dma_start(out[block * P : (block + 1) * P, g : g + n], results[:, block, g : g + n])
 
-        def multiply_first_pieces(h):
-            for i in range(2):
-                multiply(2 * h, i * PIECE, PIECE)
-            multiply(2 * h + 1, 0, 2 * PIECE)
-
         for block in range(BLOCKS):
             group_w(block)
 
@@ -171,19 +166,24 @@ def tile_attend_aq_bias_kernel(tc, cb, w, norm, bias, offs, out):
             step(0)
             step(1)
 
-        quantise_w(0)
-        multiply_first_pieces(0)
+        quantise_w(0, slice(0, HALF), w_first[:])
+        for i in range(2):
+            multiply(0, i * PIECE, PIECE)
+        multiply(1, 0, 2 * PIECE)
         middle = hold.tile([P, PIECE], F32, name="middle", tag="stage_0", align_bytes=64)
         sums[2] = middle[:]
         gather(2)
-        quantise_w(1)
-        multiply_first_pieces(1)
+        quantise_w(1, slice(0, P), w_third[:])
+        for i in range(2):
+            multiply(2, i * PIECE, PIECE)
         late = hold.tile([P, PIECE + PIECE // 2], F32, name="late", tag="stage_1", align_bytes=64)
         sums[3] = late[:, 0:PIECE]
         rounded[2] = late[:, PIECE:].bitcast(BF16)
 
         scale(2)
         gather(3)
+        quantise_w(1, slice(P, HALF), w_fourth[:])
+        multiply(3, 0, 2 * PIECE)
         place(2)
         scale(3)
         quantise_e(2)

@@ -36,20 +36,21 @@ def tile_attend_aq_bias_kernel(tc, cb, w, norm, bias, offs, out):
         ring = ctx.enter_context(tc.tile_pool(name="ring", bufs=2))
         psum = ctx.enter_context(tc.psum_pool(name="psum", bufs=8))
 
-        bias_rows = hold.tile([P, P], F32, name="bias_rows")
-        nc.gpsimd.memset(bias_rows[:], 0.0)
-        norm_runs = hold.tile([P, NORM_RUN], F32, name="norm_runs")
-        nc.scalar.dma_start(norm_runs[:], norm[0:1, :].rearrange("o (p c) -> (o p) c", c=NORM_RUN))
-        nc.scalar.dma_start(bias_rows[0:BLOCKS, :], bias.rearrange("(b p) o -> b (p o)", p=P))
+        rows = hold.tile([P, P], F32, name="rows")
+        nc.gpsimd.memset(rows[:], 0.0)
 
         offsets = hold.tile([P, O * G // LIST_ROWS], U16, name="offsets")
-        tables = {}
-        for t in range(PACK):
-            for o in range(O):
-                tables[o, t] = hold.tile([P, T], F32, name="table_%d_%d" % (o, t))
-                nc.sync.dma_start(tables[o, t][:], cb[o].rearrange("(p t) c -> p t c", t=PACK)[:, t, :])
-                if (o, t) == (0, 0):
-                    nc.sync.dma_start(offsets[:], offs)
+        planes = [cb[o].rearrange("(p t) c -> p t c", t=PACK) for o in range(O)]
+        early = hold.tile([P, LAST, T], F32, name="early")
+        nc.sync.dma_start(early[:], planes[0][:, 0:LAST, :])
+        nc.sync.dma_start(offsets[:], offs)
+        nc.sync.dma_start(rows[0:NORM_RUN, :], norm[0:1, :].rearrange("o (r c) -> (o r) c", c=P))
+        nc.sync.dma_start(rows[NORM_RUN : NORM_RUN + BLOCKS, :], bias.rearrange("(b p) o -> b (p o)", p=P))
+        tables = {(0, t): early[:, t, :] for t in range(LAST)}
+        for o, t in [(1, t) for t in range(LAST)] + [(0, LAST), (1, LAST)]:
+            table = hold.tile([P, T], F32, name="table_%d_%d" % (o, t))
+            nc.sync.dma_start(table[:], planes[o][:, t, :])
+            tables[o, t] = table[:]
         w_raw = []
         for h in range(2):
             w_raw.append(hold.tile([P, PACK, HALF], F32, name="w_raw_%d" % h))
@@ -58,20 +59,18 @@ def tile_attend_aq_bias_kernel(tc, cb, w, norm, bias, offs, out):
         ident = hold.tile([P, P], F32, name="ident")
         make_identity(nc, ident[:])
 
+        rows_turned = psum.tile([P, P], F32, name="rows_turned", tag="bank")
+        nc.tensor.transpose(rows_turned[:], rows[:], ident[:])
+        cols = hold.tile([P, NORM_RUN + BLOCKS], F32, name="cols")
+        nc.scalar.copy(cols[:], rows_turned[:, 0 : NORM_RUN + BLOCKS])
+        bias_cols = cols[:, NORM_RUN:]
         norm_all = hold.tile([P, G], F32, name="norm_all")
         per_bank = BANK // P
-        for c0 in range(0, NORM_RUN, per_bank):
+        for r0 in range(0, NORM_RUN, per_bank):
             turned = psum.tile([P, per_bank, P], F32, name="turned", tag="bank")
-            for c in range(per_bank):
-                nc.tensor.transpose(turned[:, c, :], norm_runs[:, c0 + c : c0 + c + 1].to_broadcast([P, P]), ident[:])
-            nc.scalar.copy(
-                norm_all[:].rearrange("q (p c) -> q p c", c=NORM_RUN)[:, :, c0 : c0 + per_bank],
-                turned[:].rearrange("q c p -> q p c"),
-            )
-        bias_turned = psum.tile([P, P], F32, name="bias_turned", tag="bank")
-        nc.tensor.transpose(bias_turned[:], bias_rows[:], ident[:])
-        bias_cols = hold.tile([P, BLOCKS], F32, name="bias_cols")
-        nc.scalar.copy(bias_cols[:], bias_turned[:, 0:BLOCKS])
+            for r in range(per_bank):
+                nc.tensor.transpose(turned[:, r, :], cols[:, r0 + r : r0 + r + 1].to_broadcast([P, P]), ident[:])
+            nc.scalar.copy(norm_all[:, r0 * P : (r0 + per_bank) * P], turned[:].rearrange("q r p -> q (r p)"))
 
         w_codes = [hold.tile([P, HALF], U32, name="w_codes_%d" % h, align_bytes=64) for h in range(2)]
         w_scales = [hold.tile([P, HALF], U8, name="w_scales_%d" % h, align_bytes=64) for h in range(2)]
@@ -100,12 +99,12 @@ def tile_attend_aq_bias_kernel(tc, cb, w, norm, bias, offs, out):
 
         def listed(o, t, g, n):
             entry = o * G + g
-            return tables[o, t][:].indirect(offsets[:, entry // LIST_ROWS : (entry + n) // LIST_ROWS])
+            return tables[o, t].indirect(offsets[:, entry // LIST_ROWS : (entry + n) // LIST_ROWS])
 
         for t in range(LAST):
             first = ring.tile([P, G], F32, name="first")
             both = ring.tile([P, G], F32, name="both")
-            plane = hold.tile([P, G], BF16, name="plane")
+            plane = hold.tile([P, G], BF16, name="plane", tag="plane_%d" % (t % 2))
             nc.vector.tensor_copy(first[:], listed(0, t, 0, G))
             nc.vector.tensor_tensor(both[:], listed(1, t, 0, G), first[:], ADD)
             nc.vector.tensor_tensor(plane[:], both[:], norm_all[:], MULT)
@@ -113,7 +112,7 @@ def tile_attend_aq_bias_kernel(tc, cb, w, norm, bias, offs, out):
 
         first = ring.tile([P, G], F32, name="first")
         nc.vector.tensor_copy(first[:], listed(0, LAST, 0, G))
-        plane = hold.tile([P, G], BF16, name="plane")
+        plane = hold.tile([P, G], BF16, name="plane", tag="plane_%d" % ((LAST - 1) % 2))
 
         sums = {}
         rounded = {i: plane[:, i * PIECE : (i + 1) * PIECE] for i in range(G // PIECE)}

@@ -7,6 +7,7 @@ O, D, T, G, M = 2, 512, 4096, 1024, 512
 P = 128
 PACK = 4
 LAST = PACK - 1
+EARLY = 2
 BLOCKS = M // P
 HALF = M // 2
 LIST_ROWS = 16
@@ -41,13 +42,13 @@ def tile_attend_aq_bias_kernel(tc, cb, w, norm, bias, offs, out):
 
         offsets = hold.tile([P, O * G // LIST_ROWS], U16, name="offsets")
         planes = [cb[o].rearrange("(p t) c -> p t c", t=PACK) for o in range(O)]
-        early = hold.tile([P, LAST, T], F32, name="early")
-        nc.sync.dma_start(early[:], planes[0][:, 0:LAST, :])
+        early = hold.tile([P, EARLY, T], F32, name="early")
+        nc.sync.dma_start(early[:], planes[0][:, 0:EARLY, :])
         nc.sync.dma_start(offsets[:], offs)
         nc.sync.dma_start(rows[0:NORM_RUN, :], norm[0:1, :].rearrange("o (r c) -> (o r) c", c=P))
         nc.sync.dma_start(rows[NORM_RUN : NORM_RUN + BLOCKS, :], bias.rearrange("(b p) o -> b (p o)", p=P))
-        tables = {(0, t): early[:, t, :] for t in range(LAST)}
-        for o, t in [(1, t) for t in range(LAST)] + [(0, LAST), (1, LAST)]:
+        tables = {(0, t): early[:, t, :] for t in range(EARLY)}
+        for o, t in [(1, t) for t in range(EARLY)] + [(o, t) for t in range(EARLY, PACK) for o in range(O)]:
             table = hold.tile([P, T], F32, name="table_%d_%d" % (o, t))
             nc.sync.dma_start(table[:], planes[o][:, t, :])
             tables[o, t] = table[:]
@@ -169,21 +170,23 @@ def tile_attend_aq_bias_kernel(tc, cb, w, norm, bias, offs, out):
         for i in range(2):
             multiply(0, i * PIECE, PIECE)
         multiply(1, 0, 2 * PIECE)
-        middle = hold.tile([P, PIECE], F32, name="middle", tag="stage_0", align_bytes=64)
-        sums[2] = middle[:]
+        sums[2] = w_raw[0][:, 0, :]
         gather(2)
         quantise_w(1, slice(0, P), w_third[:])
         for i in range(2):
             multiply(2, i * PIECE, PIECE)
-        late = hold.tile([P, PIECE + PIECE // 2], F32, name="late", tag="stage_1", align_bytes=64)
-        sums[3] = late[:, 0:PIECE]
-        rounded[2] = late[:, PIECE:].bitcast(BF16)
 
-        scale(2)
+        def halves(ap):
+            return ap.rearrange("p (a c) -> p a c", a=2)
+
+        product = w_raw[1][:, 0:2, 0:P]
+        nc.vector.tensor_tensor(product, halves(sums[2]), halves(norm_all[:, 2 * PIECE : 3 * PIECE]), MULT)
+        late = hold.tile([P, PIECE], F32, name="late", tag="stage_1", align_bytes=64)
+        sums[3] = late[:]
         gather(3)
         quantise_w(1, slice(P, HALF), w_fourth[:])
         multiply(3, 0, 2 * PIECE)
-        place(2)
+        nc.vector.tensor_copy(halves(e_groups[:, 2 * PIECE : 3 * PIECE, LAST]), product)
         scale(3)
         quantise_e(2)
         for block in range(BLOCKS):

@@ -137,7 +137,12 @@ def tile_attend_aq_bias_kernel(tc, cb, w, norm, bias, offs, out):
 
         results = hold.tile([P, BLOCKS, G], F32, name="results")
 
-        def multiply(block, g, n, on_vector=False):
+        out_blocks = out.rearrange("(b p) g -> p b g", p=P)
+
+        def store(block, blocks, g, n):
+            nc.sync.dma_start(out_blocks[:, block : block + blocks, g : g + n], results[:, block : block + blocks, g : g + n])
+
+        def multiply(block, g, n, on_vector=False, stored=True):
             h, b = divmod(block, 2)
             acc = psum.tile([P, n], F32, name="acc", tag="bank")
             nc.tensor.matmul_mx(
@@ -153,7 +158,8 @@ def tile_attend_aq_bias_kernel(tc, cb, w, norm, bias, offs, out):
                 nc.vector.tensor_scalar_add(results[:, block, g : g + n], acc[:], bias_cols[:, block : block + 1])
             else:
                 nc.scalar.activation(results[:, block, g : g + n], acc[:], IDENTITY, bias=bias_cols[:, block : block + 1])
-            nc.sync.dma_start(out[block * P : (block + 1) * P, g : g + n], results[:, block, g : g + n])
+            if stored:
+                store(block, 1, g, n)
 
         for block in range(BLOCKS):
             group_w(block)
@@ -189,10 +195,13 @@ def tile_attend_aq_bias_kernel(tc, cb, w, norm, bias, offs, out):
         nc.vector.tensor_copy(halves(e_groups[:, 2 * PIECE : 3 * PIECE, LAST]), product)
         scale(3)
         quantise_e(2)
-        for block in range(BLOCKS):
-            multiply(block, 2 * PIECE, PIECE)
+        for block in range(3):
+            multiply(block, 2 * PIECE, PIECE, stored=block < 2)
         place(3)
         quantise_e(3)
-        for block in range(2):
-            for lower in range(2):
-                multiply(block + 2 * lower, 3 * PIECE, PIECE, on_vector=lower == 1)
+        multiply(3, 2 * PIECE, PIECE, on_vector=True, stored=False)
+        store(2, 2, 2 * PIECE, PIECE)
+        for block in range(BLOCKS):
+            multiply(block, 3 * PIECE, PIECE, on_vector=block % 2 == 1, stored=False)
+            if block % 2 == 1:
+                store(block - 1, 2, 3 * PIECE, PIECE)

@@ -168,19 +168,19 @@ def tile_attend_aq_bias_kernel(tc, cb, w, norm, bias, offs, out):
         for i in range(2):
             sums[i] = early_sums[:, i, :]
             gather(i)
-        for step in (scale, place, quantise_e):
+        for step in (scale, place):
             step(0)
             step(1)
 
-        quantise_w(0, slice(0, HALF), w_first[:])
         for i in range(2):
+            quantise_e(i)
+            quantise_w(0, slice(i * P, (i + 1) * P), w_groups[i])
             multiply(0, i * PIECE, PIECE)
         multiply(1, 0, 2 * PIECE)
         sums[2] = w_raw[0][:, 0, :]
         gather(2)
         quantise_w(1, slice(0, P), w_third[:])
-        for i in range(2):
-            multiply(2, i * PIECE, PIECE)
+        multiply(2, 0, 2 * PIECE)
 
         def halves(ap):
             return ap.rearrange("p (a c) -> p a c", a=2)
@@ -191,7 +191,8 @@ def tile_attend_aq_bias_kernel(tc, cb, w, norm, bias, offs, out):
         sums[3] = late[:]
         gather(3)
         quantise_w(1, slice(P, HALF), w_fourth[:])
-        multiply(3, 0, 2 * PIECE)
+        for i in range(2):
+            multiply(3, i * PIECE, PIECE)
         nc.vector.tensor_copy(halves(e_groups[:, 2 * PIECE : 3 * PIECE, LAST]), product)
         scale(3)
         quantise_e(2)

@@ -26,6 +26,7 @@ U16 = mybir.dt.uint16
 U8 = mybir.dt.uint8
 FP8X4 = mybir.dt.float8_e4m3fn_x4
 IDENTITY = mybir.ActivationFunctionType.Identity
+COPY = mybir.ActivationFunctionType.Copy
 MULT = mybir.AluOpType.mult
 ADD = mybir.AluOpType.add
 
@@ -161,6 +162,8 @@ def tile_attend_aq_bias_kernel(tc, cb, w, norm, bias, offs, out):
             if stored:
                 store(block, 1, g, n)
 
+        picked = hold.tile([P, PIECE], F32, name="picked")
+        nc.scalar.activation(picked[:], listed(1, LAST, 2 * PIECE, PIECE), COPY)
         for block in range(BLOCKS):
             group_w(block)
 
@@ -178,7 +181,7 @@ def tile_attend_aq_bias_kernel(tc, cb, w, norm, bias, offs, out):
             multiply(0, i * PIECE, PIECE)
         multiply(1, 0, 2 * PIECE)
         sums[2] = w_raw[0][:, 0, :]
-        gather(2)
+        nc.vector.tensor_tensor(sums[2], picked[:], first[:, 2 * PIECE : 3 * PIECE], ADD)
         quantise_w(1, slice(0, P), w_third[:])
         multiply(2, 0, 2 * PIECE)
 

@@ -162,8 +162,8 @@ def tile_attend_aq_bias_kernel(tc, cb, w, norm, bias, offs, out):
             if stored:
                 store(block, 1, g, n)
 
-        picked = hold.tile([P, PIECE], F32, name="picked")
-        nc.scalar.activation(picked[:], listed(1, LAST, 2 * PIECE, PIECE), COPY)
+        picked = hold.tile([P, 2 * PIECE], F32, name="picked")
+        nc.scalar.activation(picked[:], listed(1, LAST, 2 * PIECE, 2 * PIECE), COPY)
         for block in range(BLOCKS):
             group_w(block)
 
@@ -181,7 +181,7 @@ def tile_attend_aq_bias_kernel(tc, cb, w, norm, bias, offs, out):
             multiply(0, i * PIECE, PIECE)
         multiply(1, 0, 2 * PIECE)
         sums[2] = w_raw[0][:, 0, :]
-        nc.vector.tensor_tensor(sums[2], picked[:], first[:, 2 * PIECE : 3 * PIECE], ADD)
+        nc.vector.tensor_tensor(sums[2], picked[:, 0:PIECE], first[:, 2 * PIECE : 3 * PIECE], ADD)
         quantise_w(1, slice(0, P), w_third[:])
         multiply(2, 0, 2 * PIECE)
 
@@ -192,7 +192,7 @@ def tile_attend_aq_bias_kernel(tc, cb, w, norm, bias, offs, out):
         nc.vector.tensor_tensor(product, halves(sums[2]), halves(norm_all[:, 2 * PIECE : 3 * PIECE]), MULT)
         late = hold.tile([P, PIECE], F32, name="late", tag="stage_1", align_bytes=64)
         sums[3] = late[:]
-        gather(3)
+        nc.vector.tensor_tensor(sums[3], picked[:, PIECE:], first[:, 3 * PIECE :], ADD)
         quantise_w(1, slice(P, HALF), w_fourth[:])
         for i in range(2):
             multiply(3, i * PIECE, PIECE)

@@ -81,9 +81,9 @@ def tile_attend_aq_bias_kernel(tc, cb, w, norm, bias, offs, out):
         w_fourth = hold.tile([P, P, PACK], BF16, name="w_fourth", align_bytes=64)
         w_groups = [w_first[:, 0:P, :], w_first[:, P:HALF, :], w_third[:], w_fourth[:]]
 
-        def group_w(block):
+        def group_w(block, copy):
             h, b = divmod(block, 2)
-            nc.scalar.copy(
+            copy(
                 w_groups[block].rearrange("p (c i) t -> p c t i", i=RUN),
                 w_raw[h][:, :, b * P : (b + 1) * P].rearrange("p t (c i) -> p c t i", i=RUN),
             )
@@ -165,7 +165,7 @@ def tile_attend_aq_bias_kernel(tc, cb, w, norm, bias, offs, out):
         picked = hold.tile([P, 2 * PIECE], F32, name="picked")
         nc.scalar.activation(picked[:], listed(1, LAST, 2 * PIECE, 2 * PIECE), COPY)
         for block in range(BLOCKS):
-            group_w(block)
+            group_w(block, nc.scalar.copy)
 
         early_sums = hold.tile([P, 2, PIECE], F32, name="early_sums")
         for i in range(2):
@@ -175,15 +175,18 @@ def tile_attend_aq_bias_kernel(tc, cb, w, norm, bias, offs, out):
             step(0)
             step(1)
 
-        for i in range(2):
-            quantise_e(i)
-            quantise_w(0, slice(i * P, (i + 1) * P), w_groups[i])
-            multiply(0, i * PIECE, PIECE)
-        multiply(1, 0, 2 * PIECE)
+        quantise_e(0)
+        for block in range(2):
+            quantise_w(0, slice(block * P, (block + 1) * P), w_groups[block])
+            multiply(block, 0, PIECE)
+        quantise_e(1)
+        for block in range(2):
+            multiply(block, PIECE, PIECE)
         sums[2] = w_raw[0][:, 0, :]
         nc.vector.tensor_tensor(sums[2], picked[:, 0:PIECE], first[:, 2 * PIECE : 3 * PIECE], ADD)
         quantise_w(1, slice(0, P), w_third[:])
-        multiply(2, 0, 2 * PIECE)
+        for i in range(2):
+            multiply(2, i * PIECE, PIECE)
 
         def halves(ap):
             return ap.rearrange("p (a c) -> p a c", a=2)
@@ -195,12 +198,15 @@ def tile_attend_aq_bias_kernel(tc, cb, w, norm, bias, offs, out):
         nc.vector.tensor_tensor(sums[3], picked[:, PIECE:], first[:, 3 * PIECE :], ADD)
         quantise_w(1, slice(P, HALF), w_fourth[:])
         for i in range(2):
-            multiply(3, i * PIECE, PIECE)
+            multiply(3, i * PIECE, PIECE, stored=False)
+        store(3, 1, 0, 2 * PIECE)
         nc.vector.tensor_copy(halves(e_groups[:, 2 * PIECE : 3 * PIECE, LAST]), product)
         scale(3)
         quantise_e(2)
         for block in range(3):
-            multiply(block, 2 * PIECE, PIECE, stored=block < 2)
+            multiply(block, 2 * PIECE, PIECE, stored=False)
+            if block == 1:
+                store(0, 2, 2 * PIECE, PIECE)
         place(3)
         quantise_e(3)
         multiply(3, 2 * PIECE, PIECE, on_vector=True, stored=False)

@@ -15,6 +15,7 @@ BANK = 512
 NORM_RUN = G // P
 PIECE = 256
 RUN = 4
+OWN = 320
 
 FLOPS = 2 * M * D * G
 BYTES = 4 * (O * D * T + D * M + G + M + M * G) + 2 * P * (O * G // LIST_ROWS)
@@ -81,9 +82,9 @@ def tile_attend_aq_bias_kernel(tc, cb, w, norm, bias, offs, out):
         w_fourth = hold.tile([P, P, PACK], BF16, name="w_fourth", align_bytes=64)
         w_groups = [w_first[:, 0:P, :], w_first[:, P:HALF, :], w_third[:], w_fourth[:]]
 
-        def group_w(block, copy):
+        def group_w(block):
             h, b = divmod(block, 2)
-            copy(
+            nc.scalar.copy(
                 w_groups[block].rearrange("p (c i) t -> p c t i", i=RUN),
                 w_raw[h][:, :, b * P : (b + 1) * P].rearrange("p t (c i) -> p c t i", i=RUN),
             )
@@ -119,9 +120,6 @@ def tile_attend_aq_bias_kernel(tc, cb, w, norm, bias, offs, out):
         sums = {}
         rounded = {i: plane[:, i * PIECE : (i + 1) * PIECE] for i in range(G // PIECE)}
 
-        def gather(i):
-            nc.vector.tensor_tensor(sums[i], listed(1, LAST, i * PIECE, PIECE), first[:, i * PIECE : (i + 1) * PIECE], ADD)
-
         def scale(i):
             nc.vector.tensor_tensor(rounded[i], sums[i], norm_all[:, i * PIECE : (i + 1) * PIECE], MULT)
 
@@ -143,34 +141,38 @@ def tile_attend_aq_bias_kernel(tc, cb, w, norm, bias, offs, out):
         def store(block, blocks, g, n):
             nc.sync.dma_start(out_blocks[:, block : block + blocks, g : g + n], results[:, block : block + blocks, g : g + n])
 
-        def multiply(block, g, n, on_vector=False, stored=True):
+        def multiply(block, i, on_vector=False, stored=True):
             h, b = divmod(block, 2)
-            acc = psum.tile([P, n], F32, name="acc", tag="bank")
+            cols = slice(i * PIECE, (i + 1) * PIECE)
+            acc = psum.tile([P, PIECE], F32, name="acc", tag="bank")
             nc.tensor.matmul_mx(
                 out=acc[:],
                 lhsT=w_codes[h][:, b * P : (b + 1) * P].bitcast(FP8X4),
                 lhsT_scale=w_scales[h][:, b * P : (b + 1) * P],
-                rhs=e_codes[:, g : g + n].bitcast(FP8X4),
-                rhs_scale=e_scales[:, g : g + n],
+                rhs=e_codes[:, cols].bitcast(FP8X4),
+                rhs_scale=e_scales[:, cols],
                 start=True,
                 stop=True,
             )
             if on_vector:
-                nc.vector.tensor_scalar_add(results[:, block, g : g + n], acc[:], bias_cols[:, block : block + 1])
+                nc.vector.tensor_scalar_add(results[:, block, cols], acc[:], bias_cols[:, block : block + 1])
             else:
-                nc.scalar.activation(results[:, block, g : g + n], acc[:], IDENTITY, bias=bias_cols[:, block : block + 1])
+                nc.scalar.activation(results[:, block, cols], acc[:], IDENTITY, bias=bias_cols[:, block : block + 1])
             if stored:
-                store(block, 1, g, n)
+                store(block, 1, i * PIECE, PIECE)
 
+        soon = hold.tile([P, 2 * PIECE - OWN], F32, name="soon")
+        nc.scalar.activation(soon[:], listed(1, LAST, OWN, 2 * PIECE - OWN), COPY)
         picked = hold.tile([P, 2 * PIECE], F32, name="picked")
         nc.scalar.activation(picked[:], listed(1, LAST, 2 * PIECE, 2 * PIECE), COPY)
         for block in range(BLOCKS):
-            group_w(block, nc.scalar.copy)
+            group_w(block)
 
-        early_sums = hold.tile([P, 2, PIECE], F32, name="early_sums")
+        early_sums = hold.tile([P, 2 * PIECE], F32, name="early_sums")
+        nc.vector.tensor_tensor(early_sums[:, 0:OWN], listed(1, LAST, 0, OWN), first[:, 0:OWN], ADD)
+        nc.vector.tensor_tensor(early_sums[:, OWN:], soon[:], first[:, OWN : 2 * PIECE], ADD)
         for i in range(2):
-            sums[i] = early_sums[:, i, :]
-            gather(i)
+            sums[i] = early_sums[:, i * PIECE : (i + 1) * PIECE]
         for step in (scale, place):
             step(0)
             step(1)
@@ -178,15 +180,15 @@ def tile_attend_aq_bias_kernel(tc, cb, w, norm, bias, offs, out):
         quantise_e(0)
         for block in range(2):
             quantise_w(0, slice(block * P, (block + 1) * P), w_groups[block])
-            multiply(block, 0, PIECE)
+            multiply(block, 0)
         quantise_e(1)
         for block in range(2):
-            multiply(block, PIECE, PIECE)
+            multiply(block, 1)
         sums[2] = w_raw[0][:, 0, :]
         nc.vector.tensor_tensor(sums[2], picked[:, 0:PIECE], first[:, 2 * PIECE : 3 * PIECE], ADD)
         quantise_w(1, slice(0, P), w_third[:])
         for i in range(2):
-            multiply(2, i * PIECE, PIECE)
+            multiply(2, i)
 
         def halves(ap):
             return ap.rearrange("p (a c) -> p a c", a=2)
@@ -198,20 +200,20 @@ def tile_attend_aq_bias_kernel(tc, cb, w, norm, bias, offs, out):
         nc.vector.tensor_tensor(sums[3], picked[:, PIECE:], first[:, 3 * PIECE :], ADD)
         quantise_w(1, slice(P, HALF), w_fourth[:])
         for i in range(2):
-            multiply(3, i * PIECE, PIECE, stored=False)
+            multiply(3, i, stored=False)
         store(3, 1, 0, 2 * PIECE)
         nc.vector.tensor_copy(halves(e_groups[:, 2 * PIECE : 3 * PIECE, LAST]), product)
         scale(3)
         quantise_e(2)
-        for block in range(3):
-            multiply(block, 2 * PIECE, PIECE, stored=False)
-            if block == 1:
-                store(0, 2, 2 * PIECE, PIECE)
+        for block in range(2):
+            multiply(block, 2, stored=False)
+        store(0, 2, 2 * PIECE, PIECE)
+        multiply(2, 2, stored=False)
         place(3)
         quantise_e(3)
-        multiply(3, 2 * PIECE, PIECE, on_vector=True, stored=False)
+        multiply(3, 2, on_vector=True, stored=False)
         store(2, 2, 2 * PIECE, PIECE)
         for block in range(BLOCKS):
-            multiply(block, 3 * PIECE, PIECE, on_vector=block % 2 == 1, stored=False)
+            multiply(block, 3, on_vector=block % 2 == 1, stored=False)
             if block % 2 == 1:
                 store(block - 1, 2, 3 * PIECE, PIECE)

@@ -188,7 +188,8 @@ def tile_attend_aq_bias_kernel(tc, cb, w, norm, bias, offs, out):
         nc.vector.tensor_tensor(sums[2], picked[:, 0:PIECE], first[:, 2 * PIECE : 3 * PIECE], ADD)
         quantise_w(1, slice(0, P), w_third[:])
         for i in range(2):
-            multiply(2, i)
+            multiply(2, i, stored=False)
+        store(2, 1, 0, 2 * PIECE)
 
         def halves(ap):
             return ap.rearrange("p (a c) -> p a c", a=2)
@@ -206,8 +207,7 @@ def tile_attend_aq_bias_kernel(tc, cb, w, norm, bias, offs, out):
         scale(3)
         quantise_e(2)
         for block in range(2):
-            multiply(block, 2, stored=False)
-        store(0, 2, 2 * PIECE, PIECE)
+            multiply(block, 2)
         multiply(2, 2, stored=False)
         place(3)
         quantise_e(3)

@@ -141,7 +141,7 @@ def tile_attend_aq_bias_kernel(tc, cb, w, norm, bias, offs, out):
         def store(block, blocks, g, n):
             nc.sync.dma_start(out_blocks[:, block : block + blocks, g : g + n], results[:, block : block + blocks, g : g + n])
 
-        def multiply(block, i, on_vector=False, stored=True):
+        def one_pass(block, i):
             h, b = divmod(block, 2)
             cols = slice(i * PIECE, (i + 1) * PIECE)
             acc = psum.tile([P, PIECE], F32, name="acc", tag="bank")
@@ -154,10 +154,17 @@ def tile_attend_aq_bias_kernel(tc, cb, w, norm, bias, offs, out):
                 start=True,
                 stop=True,
             )
+            return acc
+
+        def empty(acc, block, i, on_vector=False):
+            cols = slice(i * PIECE, (i + 1) * PIECE)
             if on_vector:
                 nc.vector.tensor_scalar_add(results[:, block, cols], acc[:], bias_cols[:, block : block + 1])
             else:
                 nc.scalar.activation(results[:, block, cols], acc[:], IDENTITY, bias=bias_cols[:, block : block + 1])
+
+        def multiply(block, i, on_vector=False, stored=True):
+            empty(one_pass(block, i), block, i, on_vector)
             if stored:
                 store(block, 1, i * PIECE, PIECE)
 
@@ -200,16 +207,17 @@ def tile_attend_aq_bias_kernel(tc, cb, w, norm, bias, offs, out):
         sums[3] = late[:]
         nc.vector.tensor_tensor(sums[3], picked[:, PIECE:], first[:, 3 * PIECE :], ADD)
         quantise_w(1, slice(P, HALF), w_fourth[:])
-        for i in range(2):
-            multiply(3, i, stored=False)
-        store(3, 1, 0, 2 * PIECE)
+        multiply(3, 0, stored=False)
+        waiting = one_pass(3, 1)
         nc.vector.tensor_copy(halves(e_groups[:, 2 * PIECE : 3 * PIECE, LAST]), product)
         scale(3)
         quantise_e(2)
+        place(3)
+        empty(waiting, 3, 1, on_vector=True)
+        store(3, 1, 0, 2 * PIECE)
         for block in range(2):
             multiply(block, 2)
         multiply(2, 2, stored=False)
-        place(3)
         quantise_e(3)
         multiply(3, 2, on_vector=True, stored=False)
         store(2, 2, 2 * PIECE, PIECE)

from contextlib import ExitStack

import concourse.mybir as mybir
from concourse.masks import make_identity

O, D, T, G, M = 2, 512, 4096, 1024, 512
P = 128
PACK = 4
LAST = PACK - 1
EARLY = 2
BLOCKS = M // P
HALF = M // 2
LIST_ROWS = 16
BANK = 512
NORM_RUN = G // P
PIECE = 256
RUN = 4
OWN = 320

FLOPS = 2 * M * D * G
BYTES = 4 * (O * D * T + D * M + G + M + M * G) + 2 * P * (O * G // LIST_ROWS)

F32 = mybir.dt.float32
BF16 = mybir.dt.bfloat16
U32 = mybir.dt.uint32
U16 = mybir.dt.uint16
U8 = mybir.dt.uint8
FP8X4 = mybir.dt.float8_e4m3fn_x4
IDENTITY = mybir.ActivationFunctionType.Identity
COPY = mybir.ActivationFunctionType.Copy
MULT = mybir.AluOpType.mult
ADD = mybir.AluOpType.add


def tile_attend_aq_bias_kernel(tc, cb, w, norm, bias, offs, out):
    nc = tc.nc
    with ExitStack() as ctx:
        hold = ctx.enter_context(tc.tile_pool(name="hold", bufs=1))
        ring = ctx.enter_context(tc.tile_pool(name="ring", bufs=2))
        psum = ctx.enter_context(tc.psum_pool(name="psum", bufs=8))

        rows = hold.tile([P, P], F32, name="rows")
        nc.gpsimd.memset(rows[:], 0.0)

        offsets = hold.tile([P, O * G // LIST_ROWS], U16, name="offsets")
        planes = [cb[o].rearrange("(p t) c -> p t c", t=PACK) for o in range(O)]
        early = hold.tile([P, EARLY, T], F32, name="early")
        nc.sync.dma_start(early[:], planes[0][:, 0:EARLY, :])
        nc.sync.dma_start(offsets[:], offs)
        nc.sync.dma_start(rows[0:NORM_RUN, :], norm[0:1, :].rearrange("o (r c) -> (o r) c", c=P))
        nc.sync.dma_start(rows[NORM_RUN : NORM_RUN + BLOCKS, :], bias.rearrange("(b p) o -> b (p o)", p=P))
        tables = {(0, t): early[:, t, :] for t in range(EARLY)}
        for o, t in [(1, t) for t in range(EARLY)] + [(o, t) for t in range(EARLY, PACK) for o in range(O)]:
            table = hold.tile([P, T], F32, name="table_%d_%d" % (o, t))
            nc.sync.dma_start(table[:], planes[o][:, t, :])
            tables[o, t] = table[:]
        w_raw = []
        for h in range(2):
            w_raw.append(hold.tile([P, PACK, HALF], F32, name="w_raw_%d" % h))
            nc.sync.dma_start(w_raw[h][:], w.rearrange("(p t) m -> p t m", t=PACK)[:, :, h * HALF : (h + 1) * HALF])

        ident = hold.tile([P, P], F32, name="ident")
        make_identity(nc, ident[:])

        rows_turned = psum.tile([P, P], F32, name="rows_turned", tag="bank")
        nc.tensor.transpose(rows_turned[:], rows[:], ident[:])
        cols = hold.tile([P, NORM_RUN + BLOCKS], F32, name="cols")
        nc.scalar.copy(cols[:], rows_turned[:, 0 : NORM_RUN + BLOCKS])
        bias_cols = cols[:, NORM_RUN:]
        norm_all = hold.tile([P, G], F32, name="norm_all")
        per_bank = BANK // P
        for r0 in range(0, NORM_RUN, per_bank):
            turned = psum.tile([P, per_bank, P], F32, name="turned", tag="bank")
            for r in range(per_bank):
                nc.tensor.transpose(turned[:, r, :], cols[:, r0 + r : r0 + r + 1].to_broadcast([P, P]), ident[:])
            nc.scalar.copy(norm_all[:, r0 * P : (r0 + per_bank) * P], turned[:].rearrange("q r p -> q (r p)"))

        w_codes = [hold.tile([P, HALF], U32, name="w_codes_%d" % h, align_bytes=64) for h in range(2)]
        w_scales = [hold.tile([P, HALF], U8, name="w_scales_%d" % h, align_bytes=64) for h in range(2)]
        w_first = hold.tile([P, HALF, PACK], BF16, name="w_first", tag="stage_0", align_bytes=64)
        w_third = hold.tile([P, P, PACK], BF16, name="w_third", tag="stage_1", align_bytes=64)
        w_fourth = hold.tile([P, P, PACK], BF16, name="w_fourth", align_bytes=64)
        w_groups = [w_first[:, 0:P, :], w_first[:, P:HALF, :], w_third[:], w_fourth[:]]

        def group_w(block):
            h, b = divmod(block, 2)
            nc.scalar.copy(
                w_groups[block].rearrange("p (c i) t -> p c t i", i=RUN),
                w_raw[h][:, :, b * P : (b + 1) * P].rearrange("p t (c i) -> p c t i", i=RUN),
            )

        def quantise_w(h, cols, groups):
            nc.vector.quantize_mx(
                out=w_codes[h][:, cols].bitcast(FP8X4),
                scales=w_scales[h][:, cols],
                in_=groups.rearrange("p m t -> p (m t)"),
            )

        e_groups = hold.tile([P, G, PACK], BF16, name="e_groups", align_bytes=64)
        e_codes = hold.tile([P, G], U32, name="e_codes", align_bytes=64)
        e_scales = hold.tile([P, G], U8, name="e_scales", align_bytes=64)

        def listed(o, t, g, n):
            entry = o * G + g
            return tables[o, t].indirect(offsets[:, entry // LIST_ROWS : (entry + n) // LIST_ROWS])

        for t in range(LAST):
            first = ring.tile([P, G], F32, name="first")
            both = ring.tile([P, G], F32, name="both")
            plane = hold.tile([P, G], BF16, name="plane", tag="plane_%d" % (t % 2))
            nc.vector.tensor_copy(first[:], listed(0, t, 0, G))
            nc.vector.tensor_tensor(both[:], listed(1, t, 0, G), first[:], ADD)
            nc.vector.tensor_tensor(plane[:], both[:], norm_all[:], MULT)
            nc.scalar.copy(e_groups[:, :, t], plane[:])

        first = ring.tile([P, G], F32, name="first")
        nc.vector.tensor_copy(first[:], listed(0, LAST, 0, G))
        plane = hold.tile([P, G], BF16, name="plane", tag="plane_%d" % ((LAST - 1) % 2))

        sums = {}
        rounded = {i: plane[:, i * PIECE : (i + 1) * PIECE] for i in range(G // PIECE)}

        def scale(i):
            nc.vector.tensor_tensor(rounded[i], sums[i], norm_all[:, i * PIECE : (i + 1) * PIECE], MULT)

        def place(i):
            nc.vector.tensor_copy(e_groups[:, i * PIECE : (i + 1) * PIECE, LAST], rounded[i])

        def quantise_e(i):
            cols = slice(i * PIECE, (i + 1) * PIECE)
            nc.vector.quantize_mx(
                out=e_codes[:, cols].bitcast(FP8X4),
                scales=e_scales[:, cols],
                in_=e_groups[:, cols, :].rearrange("p g t -> p (g t)"),
            )

        results = hold.tile([P, BLOCKS, G], F32, name="results")

        out_blocks = out.rearrange("(b p) g -> p b g", p=P)

        def store(block, blocks, g, n):
            nc.sync.dma_start(out_blocks[:, block : block + blocks, g : g + n], results[:, block : block + blocks, g : g + n])

        def one_pass(block, i):
            h, b = divmod(block, 2)
            cols = slice(i * PIECE, (i + 1) * PIECE)
            acc = psum.tile([P, PIECE], F32, name="acc", tag="bank")
            nc.tensor.matmul_mx(
                out=acc[:],
                lhsT=w_codes[h][:, b * P : (b + 1) * P].bitcast(FP8X4),
                lhsT_scale=w_scales[h][:, b * P : (b + 1) * P],
                rhs=e_codes[:, cols].bitcast(FP8X4),
                rhs_scale=e_scales[:, cols],
                start=True,
                stop=True,
            )
            return acc

        def empty(acc, block, i, on_vector=False):
            cols = slice(i * PIECE, (i + 1) * PIECE)
            if on_vector:
                nc.vector.tensor_scalar_add(results[:, block, cols], acc[:], bias_cols[:, block : block + 1])
            else:
                nc.scalar.activation(results[:, block, cols], acc[:], IDENTITY, bias=bias_cols[:, block : block + 1])

        def multiply(block, i, on_vector=False, stored=True):
            empty(one_pass(block, i), block, i, on_vector)
            if stored:
                store(block, 1, i * PIECE, PIECE)

        soon = hold.tile([P, 2 * PIECE - OWN], F32, name="soon")
        nc.scalar.activation(soon[:], listed(1, LAST, OWN, 2 * PIECE - OWN), COPY)
        picked = hold.tile([P, 2 * PIECE], F32, name="picked")
        nc.scalar.activation(picked[:], listed(1, LAST, 2 * PIECE, 2 * PIECE), COPY)
        for block in range(BLOCKS):
            group_w(block)

        early_sums = hold.tile([P, 2 * PIECE], F32, name="early_sums")
        nc.vector.tensor_tensor(early_sums[:, 0:OWN], listed(1, LAST, 0, OWN), first[:, 0:OWN], ADD)
        nc.vector.tensor_tensor(early_sums[:, OWN:], soon[:], first[:, OWN : 2 * PIECE], ADD)
        for i in range(2):
            sums[i] = early_sums[:, i * PIECE : (i + 1) * PIECE]
        for step in (scale, place):
            step(0)
            step(1)

        quantise_e(0)
        for block in range(2):
            quantise_w(0, slice(block * P, (block + 1) * P), w_groups[block])
            multiply(block, 0)
        quantise_e(1)
        for block in range(2):
            multiply(block, 1)
        sums[2] = w_raw[0][:, 0, :]
        nc.vector.tensor_tensor(sums[2], picked[:, 0:PIECE], first[:, 2 * PIECE : 3 * PIECE], ADD)
        quantise_w(1, slice(0, P), w_third[:])
        for i in range(2):
            multiply(2, i, stored=False)
        store(2, 1, 0, 2 * PIECE)

        def halves(ap):
            return ap.rearrange("p (a c) -> p a c", a=2)

        product = w_raw[1][:, 0:2, 0:P]
        nc.vector.tensor_tensor(product, halves(sums[2]), halves(norm_all[:, 2 * PIECE : 3 * PIECE]), MULT)
        late = hold.tile([P, PIECE], F32, name="late", tag="stage_1", align_bytes=64)
        sums[3] = late[:]
        nc.vector.tensor_tensor(sums[3], picked[:, PIECE:], first[:, 3 * PIECE :], ADD)
        quantise_w(1, slice(P, HALF), w_fourth[:])
        multiply(3, 0, stored=False)
        waiting = one_pass(3, 1)
        nc.vector.tensor_copy(halves(e_groups[:, 2 * PIECE : 3 * PIECE, LAST]), product)
        scale(3)
        quantise_e(2)
        place(3)
        empty(waiting, 3, 1, on_vector=True)
        store(3, 1, 0, 2 * PIECE)
        for block in range(2):
            multiply(block, 2)
        multiply(2, 2, stored=False)
        quantise_e(3)
        multiply(3, 2, on_vector=True, stored=False)
        store(2, 2, 2 * PIECE, PIECE)
        for block in range(BLOCKS):
            multiply(block, 3, on_vector=block % 2 == 1, stored=False)
            if block % 2 == 1:
                store(block - 1, 2, 3 * PIECE, PIECE)
